import numpy as np
import ml_dtypes


def mxq(x, axis, fmt="e4m3"):
    dtype, down = {"e4m3": (ml_dtypes.float8_e4m3fn, 7), "e5m2": (ml_dtypes.float8_e5m2, 14)}[fmt]
    v = np.moveaxis(np.asarray(x, np.float32).astype(ml_dtypes.bfloat16).astype(np.float64), axis, -1)
    blocks = v.reshape(v.shape[:-1] + (-1, 32))
    amax = np.abs(blocks).max(-1, keepdims=True)
    byte = np.maximum(np.where(amax > 0, np.frexp(amax)[1] - 1 + 127, 0) - down, 1)
    scale = np.exp2(byte - 127.0)
    codes = (blocks / scale).astype(np.float32).astype(dtype).astype(np.float64)
    return np.moveaxis((codes * scale).reshape(v.shape), -1, axis)


WIDE = False


def mx_kscale(k):
    if not WIDE:
        return np.ones(k)
    levels = np.array([10, -10, 5, -5, 0])
    if k % 512:
        return np.exp2(np.random.permutation(np.resize(levels, k // 32))).repeat(32)
    a = np.empty((k // 512, 16))
    for p in range(k // 512):
        a[p, :8] = np.random.permutation(np.resize(levels, 8))
        for g in range(8):
            far = levels[np.abs(levels - a[p, g]) >= 10]
            a[p, g + 8] = far[np.random.randint(len(far))]
    return np.exp2(a.ravel()).repeat(32)


def f64(x):
    return np.asarray(x).astype(np.float64)


def striped(idx):
    return np.tile(np.asarray(idx).reshape(-1, 16).T, (8, 1)).astype(np.uint16)


def unstriped(offs):
    return offs[:16].T.reshape(-1).astype(np.int64)


E2M1 = np.array([0.0, 0.5, 1.0, 1.5, 2.0, 3.0, 4.0, 6.0, -0.0, -0.5, -1.0, -1.5, -2.0, -3.0, -4.0, -6.0])


def pack_weight(w, fmt):
    k, n = w.shape
    w = f64(np.asarray(w, np.float32).astype(ml_dtypes.bfloat16)).reshape(k // 32, 32, n)
    amax = np.abs(w).max(1)
    if fmt == "e4m3":
        byte = np.frexp(amax)[1] - 1 + 127 - 7
    else:
        mant, ex = np.frexp(amax / 6.0)
        byte = np.where(mant > 0.5, ex, ex - 1) + 127
    byte = np.clip(np.where(amax > 0, byte, 1), 1, 254)
    scaled = (w * np.exp2(127.0 - byte)[:, None, :]).reshape(k, n).astype(np.float32)
    by_word = np.ascontiguousarray(scaled.reshape(k // 512, 128, 4, n).transpose(0, 1, 3, 2))
    if fmt == "e4m3":
        words = by_word.astype(ml_dtypes.float8_e4m3fn).view(np.uint8)
    else:
        c = by_word.astype(ml_dtypes.float4_e2m1fn).view(np.uint8) & 0xF
        words = (c[..., 0::2] | (c[..., 1::2] << 4)).reshape(k // 512, 128, 2 * n)
    return np.ascontiguousarray(words), np.ascontiguousarray(byte.astype(np.uint8).reshape(k // 512, 16, n))


def unpack_weight(words, scales, fmt):
    g, _, n = scales.shape
    words = np.ascontiguousarray(words).reshape(g, 128, n, -1)
    if fmt == "e4m3":
        vals = words.view(ml_dtypes.float8_e4m3fn).astype(np.float64)
    else:
        nib = np.empty((g, 128, n, 4), np.uint8)
        nib[..., 0::2] = words & 0xF
        nib[..., 1::2] = words >> 4
        vals = E2M1[nib]
    vals = vals * np.repeat(np.exp2(scales.astype(np.float64) - 127.0), 8, axis=1)[..., None]
    return vals.transpose(0, 1, 3, 2).reshape(g * 512, n)


D, E, T, I, Q, G = 512, 512, 2048, 512, 128, 64


def setup_inputs():
    n = np.random.standard_normal
    idx = np.random.permutation(T)[:I]
    fd = mx_kscale(D)
    fe = mx_kscale(E)
    keysp = pack_weight(n((D, T)) / fd[:, None], "e4m3")
    valsp = pack_weight(n((E, T)) / fe[:, None], "e4m3")
    return {
        "query": (n((D, Q)) * 0.6 / np.sqrt(D) * fd[:, None]).astype(np.float32),
        "keys_words": keysp[0],
        "keys_scales": keysp[1],
        "pw": (np.random.uniform(0.5, 1.6, (Q, 1))).astype(np.float32),
        "gout": (n((E, Q)) * 1 / np.sqrt(E) * fe[:, None]).astype(np.float32),
        "vals_words": valsp[0],
        "vals_scales": valsp[1],
        "old": (0.5 * n((Q, T))).astype(np.float32),
        "offs": striped(idx),
    }


def reference(query, keys_words, keys_scales, pw, gout, vals_words, vals_scales, old, offs):
    idx = unstriped(offs)
    keysu = unpack_weight(keys_words, keys_scales, "e4m3")
    valsu = unpack_weight(vals_words, vals_scales, "e4m3")
    queryq = mxq(f64(query), 0, "e4m3")
    keysidxg = keysu[:, idx]
    a = queryq.T @ keysidxg
    x1 = np.exp(a)
    s = x1.reshape(Q, G, I // G).sum(axis=2)
    z = np.sum(x1, axis=1, keepdims=True)
    ls = np.log(s)
    lr = np.repeat(ls, I // G, axis=1)
    sr = np.repeat(s, I // G, axis=1)
    goutq = mxq(f64(gout), 0, "e4m3")
    valsidxg = valsu[:, idx]
    c0 = goutq.T @ valsidxg
    dsr = c0 / z * np.exp((a - lr) * f64(pw))
    dlr = c0 / z * sr * np.exp((a - lr) * f64(pw)) * f64(pw) * (-1.0)
    dls = dlr.reshape(Q, G, I // G).sum(axis=2)
    dz = np.sum(c0 * np.exp((a - lr) * f64(pw)) * sr / np.square(z) * (-1.0), axis=1, keepdims=True)
    ds = dsr.reshape(Q, G, I // G).sum(axis=2) + dls / s
    r1 = np.repeat(ds, I // G, axis=1)
    dx1 = dz + r1
    da = c0 / z * sr * np.exp((a - lr) * f64(pw)) * f64(pw) + dx1 * x1
    gs = da * 128.0
    gf = np.zeros((Q, T))
    gf[:, idx] = gs
    y = f64(old) + gf
    return y

@@ -1,0 +1,246 @@
+import math
+from contextlib import ExitStack
+
+import concourse.mybir as mybir
+
+F32 = mybir.dt.float32
+BF16 = mybir.dt.bfloat16
+I32 = mybir.dt.int32
+U32 = mybir.dt.uint32
+U16 = mybir.dt.uint16
+U8 = mybir.dt.uint8
+FP8X4 = mybir.dt.float8_e4m3fn_x4
+ALU = mybir.AluOpType
+ACT = mybir.ActivationFunctionType
+AX = mybir.AxisListType
+
+P = 128
+D, E, T, I, Q, G = 512, 512, 2048, 512, 128, 64
+PAGE = I // G
+HALVES = 2
+SLOTS = I // HALVES
+PAGES = G // HALVES
+GAIN = 128.0
+STORE_WIDTHS = [256, 512, 512, 512, 256]
+
+FLOPS = 2 * Q * I * (D + E)
+
+GUESS_TOP = 2.28125
+GUESS_DROP = 3.08
+GUESS_RATE = 0.318
+GUESS_REACH = 0.045
+LOG_DEGREE = 5
+
+
+def log_polynomial(reach, degree):
+    lo, hi = math.exp(-reach), math.exp(reach)
+    nodes = [(lo + hi) / 2 + (hi - lo) / 2 * math.cos(math.pi * (k + 0.5) / (degree + 1)) for k in range(degree + 1)]
+    diffs = [math.log(node) for node in nodes]
+    for level in range(1, degree + 1):
+        diffs = diffs[:level] + [(diffs[k] - diffs[k - 1]) / (nodes[k] - nodes[k - level]) for k in range(level, degree + 1)]
+    coeffs = [diffs[degree]]
+    for k in reversed(range(degree)):
+        coeffs = [up - nodes[k] * low for up, low in zip([diffs[k]] + coeffs, coeffs + [0.0])]
+    return coeffs
+
+
+LOG_COEFFS = log_polynomial(GUESS_REACH, LOG_DEGREE)
+SERIES_LEAD = LOG_COEFFS[LOG_DEGREE]
+SERIES_STEPS = [LOG_COEFFS[k] / SERIES_LEAD for k in reversed(range(1, LOG_DEGREE))]
+SERIES_CONST = LOG_COEFFS[0]
+
+
+def tile_attend_bsharedpower_s_kernel(tc, query, keys_words, keys_scales, pw, gout, vals_words, vals_scales, old, offs, out):
+    nc = tc.nc
+    with ExitStack() as ctx:
+        sb = ctx.enter_context(tc.tile_pool(name="sb", bufs=1))
+        ps = ctx.enter_context(tc.psum_pool(name="ps", bufs=1))
+
+        def tile(shape, dtype, name, tag=None):
+            return sb.tile(shape, dtype, name=name, tag=tag or name, align_bytes=64)
+
+        offsets = sb.tile([P, I // 16], U16, name="offsets")
+        key_bytes = tile([P, T], U8, "key_bytes")
+        val_bytes = tile([P, T], U8, "val_bytes")
+        key_words = tile([P, T], I32, "key_words")
+        val_words = tile([P, T], I32, "val_words")
+        query_raw = tile([P, 4, Q], F32, "query_raw")
+        power = tile([P, 1], F32, "power")
+        placed = tile([P, T], F32, "placed")
+
+        def load_scale_rows(dst, src, queues):
+            for quad in range(4):
+                queues[quad].dma_start(out=dst[32 * quad : 32 * quad + 4, :].bitcast(I32), in_=src[0, 4 * quad : 4 * quad + 4, :].bitcast(I32))
+
+        def load_words(dst, src):
+            nc.sync.dma_start(out=dst[:], in_=src[0].rearrange("p n t -> p (n t)").bitcast(I32))
+
+        def load_rows(dst, src, queue):
+            queue.dma_start(out=dst[:], in_=src.rearrange("(p j) w -> p j w", j=4))
+
+        nc.vector.memset(key_bytes[:].bitcast(I32), 0)
+        nc.vector.memset(val_bytes[:].bitcast(I32), 0)
+        nc.sync.dma_start(offsets[:], offs)
+        load_rows(query_raw, query, nc.sync)
+        load_words(key_words, keys_words)
+        load_words(val_words, vals_words)
+        load_scale_rows(key_bytes, keys_scales, [nc.scalar] * 4)
+        load_scale_rows(val_bytes, vals_scales, [nc.scalar, nc.scalar, nc.gpsimd, nc.gpsimd])
+        nc.gpsimd.dma_start(out=power[:], in_=pw)
+        nc.vector.memset(placed[:], 0.0)
+
+        def cast(raw, name, copy):
+            grouped = tile([P, Q, 4], BF16, name)
+            copy(out=grouped[:], in_=raw[:].rearrange("p j w -> p w j"))
+            return grouped
+
+        def quantize(grouped, name):
+            codes = tile([P, Q], U32, name + "_codes")
+            scales = tile([P, Q], U8, name + "_scales")
+            nc.vector.quantize_mx(out=codes[:].bitcast(FP8X4), scales=scales[:], in_=grouped[:].rearrange("p w j -> p (w j)"))
+            return codes, scales
+
+        def gather_bytes(window, name):
+            picked = tile([P, I], U8, name)
+            nc.vector.tensor_copy(picked[:], window[:].indirect(offsets[:]))
+            return picked
+
+        def gather_words(window, half, name):
+            picked = tile([P, SLOTS], U32, name + str(half))
+            cols = SLOTS // 16
+            nc.vector.tensor_copy(picked[:], window[:].bitcast(U32).indirect(offsets[:, half * cols : (half + 1) * cols]))
+            return picked
+
+        def product(rows, words, scale_bytes, half, name):
+            bank = ps.tile([P, SLOTS], F32, name=name + str(half))
+            nc.tensor.matmul_mx(
+                out=bank[:],
+                lhsT=rows[0][:].bitcast(FP8X4),
+                lhsT_scale=rows[1][:],
+                rhs=words[:].bitcast(FP8X4),
+                rhs_scale=scale_bytes[:, half * SLOTS : (half + 1) * SLOTS],
+                start=True,
+                stop=True,
+            )
+            return bank
+
+        def slots(t, half):
+            return t[:, half * SLOTS : (half + 1) * SLOTS]
+
+        def pages(t, half):
+            return t[:, half * PAGES : (half + 1) * PAGES]
+
+        def by_page(ap):
+            return ap.rearrange("p (g j) -> p g j", j=PAGE)
+
+        def spread(ap, n):
+            return ap.unsqueeze(2).to_broadcast([P, n, PAGE])
+
+        neg_power = tile([P, 1], F32, "neg_power")
+        gains = tile([P, 2], F32, "gains")
+        nc.scalar.activation(neg_power[:], power[:], ACT.Copy, scale=-1.0)
+        nc.scalar.activation(gains[:, 0:1], power[:], ACT.Copy, scale=-GAIN, bias=GAIN)
+        nc.scalar.activation(gains[:, 1:2], power[:], ACT.Copy, scale=GAIN)
+
+        query_mx = quantize(cast(query_raw, "query_bf", nc.vector.tensor_copy), "query")
+        key_scale = gather_bytes(key_bytes, "key_scale")
+        val_scale = gather_bytes(val_bytes, "val_scale")
+        gout_raw = tile([P, 4, Q], F32, "gout_raw", tag="key_bytes")
+        load_rows(gout_raw, gout, nc.scalar)
+        gout_bf = cast(gout_raw, "gout_bf", nc.scalar.copy)
+
+        page_max = tile([P, G], F32, "page_max")
+        rel = tile([P, I], F32, "rel")
+        x = tile([P, I], F32, "x")
+        xp = tile([P, I], F32, "xp")
+        page_sum = tile([P, G], F32, "page_sum")
+
+        keys = [gather_words(key_words, h, "keys") for h in range(HALVES)]
+        old_sb = tile([P, T], F32, "old_sb", tag="key_words")
+        nc.sync.dma_start(out=old_sb[:], in_=old)
+        scores = [product(query_mx, keys[h], key_scale, h, "scores") for h in range(HALVES)]
+        for h in range(HALVES):
+            nc.vector.tensor_reduce(out=pages(page_max, h), in_=by_page(scores[h][:]), axis=AX.X, op=ALU.max)
+        for h in range(HALVES):
+            nc.vector.tensor_tensor(by_page(slots(rel, h)), by_page(scores[h][:]), spread(pages(page_max, h), PAGES), ALU.subtract)
+        for h in range(HALVES):
+            nc.scalar.activation(slots(x, h), slots(rel, h), ACT.Exp)
+        for h in range(HALVES):
+            nc.scalar.activation(slots(xp, h), slots(rel, h), ACT.Exp, scale=power[:])
+
+        neg_max = tile([P, 1], F32, "neg_max")
+        nc.vector.tensor_reduce(out=neg_max[:], in_=page_max[:], axis=AX.X, op=ALU.max, negate=True)
+        weight = tile([P, G], F32, "weight")
+        nc.scalar.activation(weight[:], page_max[:], ACT.Exp, bias=neg_max[:])
+        gout_mx = quantize(gout_bf, "gout")
+
+        vals = []
+        for h in range(HALVES):
+            nc.vector.tensor_reduce(out=pages(page_sum, h), in_=by_page(slots(x, h)), axis=AX.X, op=ALU.add)
+            vals.append(gather_words(val_words, h, "vals"))
+        grads = [product(gout_mx, vals[h], val_scale, h, "grads") for h in range(HALVES)]
+
+        inv_guess = tile([P, G], F32, "inv_guess")
+        guess = tile([P, G], F32, "guess")
+        decay = tile([P, G], F32, "decay")
+        nc.scalar.activation(decay[:], page_sum[:], ACT.Exp, scale=-GUESS_RATE)
+        nc.scalar.activation(inv_guess[:], decay[:], ACT.Exp, scale=GUESS_DROP, bias=-GUESS_TOP)
+        nc.scalar.activation(guess[:], decay[:], ACT.Copy, scale=-GUESS_DROP, bias=GUESS_TOP + SERIES_CONST)
+
+        pair = tile([P, 2, G], F32, "pair")
+        mass = pair[:, 1, :]
+        z = tile([P, 1], F32, "z")
+        inv_z = tile([P, 1], F32, "inv_z")
+        gains_z = tile([P, 2], F32, "gains_z")
+        cross_gain = tile([P, 1], F32, "cross_gain")
+        u = tile([P, G], F32, "u")
+        cx = tile([P, I], F32, "cx")
+        page_grad = tile([P, G], F32, "page_grad")
+        horner = [tile([P, G], F32, "horner" + str(k)) for k in range(len(SERIES_STEPS))]
+        log_sum = tile([P, G], F32, "log_sum")
+
+        def series_step(k):
+            src = u if k == 0 else horner[k - 1]
+            nc.vector.scalar_tensor_tensor(horner[k][:], src[:], SERIES_STEPS[k], u[:], ALU.add, ALU.mult)
+
+        nc.vector.scalar_tensor_tensor(mass, page_sum[:], 1.0, weight[:], ALU.mult, ALU.mult, accum_out=z[:])
+        nc.vector.tensor_tensor(u[:], page_sum[:], inv_guess[:], ALU.mult)
+        nc.vector.reciprocal(inv_z[:], z[:])
+        series_step(0)
+        nc.vector.tensor_tensor(slots(cx, 0), grads[0][:], slots(xp, 0), ALU.mult)
+        series_step(1)
+        nc.vector.tensor_tensor(slots(cx, 1), grads[1][:], slots(xp, 1), ALU.mult)
+        series_step(2)
+        nc.vector.tensor_reduce(out=pages(page_grad, 0), in_=by_page(slots(cx, 0)), axis=AX.X, op=ALU.add)
+        series_step(3)
+        nc.vector.tensor_reduce(out=pages(page_grad, 1), in_=by_page(slots(cx, 1)), axis=AX.X, op=ALU.add)
+        nc.vector.scalar_tensor_tensor(log_sum[:], horner[-1][:], SERIES_LEAD, guess[:], ALU.mult, ALU.add)
+        nc.scalar.activation(gains_z[:], gains[:], ACT.Copy, scale=inv_z[:])
+        nc.scalar.activation(cross_gain[:], inv_z[:], ACT.Copy, scale=-GAIN)
+        r = tile([P, G], F32, "r")
+        nc.scalar.activation(r[:], log_sum[:], ACT.Exp, scale=neg_power[:])
+
+        cross = tile([P, G], F32, "cross")
+        nc.vector.scalar_tensor_tensor(pair[:, 0, :], page_grad[:], gains_z[:, 0:1], weight[:], ALU.mult, ALU.mult)
+        nc.vector.scalar_tensor_tensor(cross[:], page_grad[:], cross_gain[:], mass, ALU.mult, ALU.mult)
+
+        pair_r = tile([P, 2, G], F32, "pair_r")
+        cross_r = tile([P, G], F32, "cross_r")
+        row_term = tile([P, 1], F32, "row_term")
+        page_term = tile([P, G], F32, "page_term")
+        own = tile([P, I], F32, "own")
+        shared = tile([P, I], F32, "shared")
+        nc.vector.scalar_tensor_tensor(cross_r[:], r[:], inv_z[:], cross[:], ALU.mult, ALU.mult, accum_out=row_term[:])
+        nc.vector.tensor_tensor(pair_r[:], pair[:], r[:].unsqueeze(1).to_broadcast([P, 2, G]), ALU.mult)
+        nc.vector.scalar_tensor_tensor(page_term[:], weight[:], row_term[:], pair_r[:, 0, :], ALU.mult, ALU.add)
+        nc.vector.scalar_tensor_tensor(by_page(own[:]), by_page(cx[:]), gains_z[:, 1:2], spread(pair_r[:, 1, :], G), ALU.mult, ALU.mult)
+        nc.vector.tensor_tensor(by_page(shared[:]), by_page(x[:]), spread(page_term[:], G), ALU.mult)
+        nc.vector.tensor_tensor(placed[:].indirect(offsets[:]), own[:], shared[:], ALU.add)
+
+        start = 0
+        for k, width in enumerate(STORE_WIDTHS):
+            cols = slice(start, start + width)
+            total = tile([P, width], F32, "total" + str(k))
+            nc.vector.tensor_tensor(total[:], placed[:, cols], old_sb[:, cols], ALU.add)
+            nc.sync.dma_start(out=out[:, cols], in_=total[:])
+            start = start + width

@@ -65,12 +65,14 @@ def tile_attend_bsharedpower_s_kernel(tc, query, keys_words, keys_scales, pw, go
         key_words = tile([P, T], I32, "key_words")
         val_words = tile([P, T], I32, "val_words")
         query_raw = tile([P, 4, Q], F32, "query_raw")
+        gout_raw = tile([P, 4, Q], F32, "gout_raw")
+        old_sb = tile([P, T], F32, "old_sb")
         power = tile([P, 1], F32, "power")
         placed = tile([P, T], F32, "placed")
 
-        def load_scale_rows(dst, src, queues):
+        def load_scale_rows(dst, src, queue, first):
             for quad in range(4):
-                queues[quad].dma_start(out=dst[32 * quad : 32 * quad + 4, :].bitcast(I32), in_=src[0, 4 * quad : 4 * quad + 4, :].bitcast(I32))
+                queue.dma_start(out=dst[32 * quad + first : 32 * quad + first + 4, :].bitcast(I32), in_=src[0, 4 * quad : 4 * quad + 4, :].bitcast(I32))
 
         def load_words(dst, src):
             nc.sync.dma_start(out=dst[:], in_=src[0].rearrange("p n t -> p (n t)").bitcast(I32))
@@ -82,11 +84,13 @@ def tile_attend_bsharedpower_s_kernel(tc, query, keys_words, keys_scales, pw, go
         nc.vector.memset(val_bytes[:].bitcast(I32), 0)
         nc.sync.dma_start(offsets[:], offs)
         load_rows(query_raw, query, nc.sync)
+        load_scale_rows(key_bytes, keys_scales, nc.sync, 0)
         load_words(key_words, keys_words)
+        load_scale_rows(val_bytes, vals_scales, nc.scalar, 4)
+        load_rows(gout_raw, gout, nc.sync)
+        nc.sync.dma_start(out=power[:], in_=pw)
         load_words(val_words, vals_words)
-        load_scale_rows(key_bytes, keys_scales, [nc.scalar] * 4)
-        load_scale_rows(val_bytes, vals_scales, [nc.scalar, nc.scalar, nc.gpsimd, nc.gpsimd])
-        nc.gpsimd.dma_start(out=power[:], in_=pw)
+        nc.sync.dma_start(out=old_sb[:], in_=old)
         nc.vector.memset(placed[:], 0.0)
 
         def cast(raw, name, copy):
@@ -105,20 +109,20 @@ def tile_attend_bsharedpower_s_kernel(tc, query, keys_words, keys_scales, pw, go
             nc.vector.tensor_copy(picked[:], window[:].indirect(offsets[:]))
             return picked
 
-        def gather_words(window, half, name):
-            picked = tile([P, SLOTS], U32, name + str(half))
+        def gather_words(window, half, name, tag=None):
+            picked = tile([P, SLOTS], U32, name + str(half), tag)
             cols = SLOTS // 16
             nc.vector.tensor_copy(picked[:], window[:].bitcast(U32).indirect(offsets[:, half * cols : (half + 1) * cols]))
             return picked
 
-        def product(rows, words, scale_bytes, half, name):
+        def product(rows, words, scale_bytes, first, half, name):
             bank = ps.tile([P, SLOTS], F32, name=name + str(half))
             nc.tensor.matmul_mx(
                 out=bank[:],
                 lhsT=rows[0][:].bitcast(FP8X4),
                 lhsT_scale=rows[1][:],
                 rhs=words[:].bitcast(FP8X4),
-                rhs_scale=scale_bytes[:, half * SLOTS : (half + 1) * SLOTS],
+                rhs_scale=scale_bytes[first:, half * SLOTS : (half + 1) * SLOTS],
                 start=True,
                 stop=True,
             )
@@ -136,18 +140,17 @@ def tile_attend_bsharedpower_s_kernel(tc, query, keys_words, keys_scales, pw, go
         def spread(ap, n):
             return ap.unsqueeze(2).to_broadcast([P, n, PAGE])
 
+        query_bf = cast(query_raw, "query_bf", nc.scalar.copy)
+        key_scale = gather_bytes(key_bytes, "key_scale")
+        query_mx = quantize(query_bf, "query")
+        val_scale = gather_bytes(val_bytes, "val_scale")
+        gout_bf = cast(gout_raw, "gout_bf", nc.scalar.copy)
+
         neg_power = tile([P, 1], F32, "neg_power")
         gains = tile([P, 2], F32, "gains")
         nc.scalar.activation(neg_power[:], power[:], ACT.Copy, scale=-1.0)
         nc.scalar.activation(gains[:, 0:1], power[:], ACT.Copy, scale=-GAIN, bias=GAIN)
         nc.scalar.activation(gains[:, 1:2], power[:], ACT.Copy, scale=GAIN)
-
-        query_mx = quantize(cast(query_raw, "query_bf", nc.vector.tensor_copy), "query")
-        key_scale = gather_bytes(key_bytes, "key_scale")
-        val_scale = gather_bytes(val_bytes, "val_scale")
-        gout_raw = tile([P, 4, Q], F32, "gout_raw", tag="key_bytes")
-        load_rows(gout_raw, gout, nc.scalar)
-        gout_bf = cast(gout_raw, "gout_bf", nc.scalar.copy)
 
         page_max = tile([P, G], F32, "page_max")
         rel = tile([P, I], F32, "rel")
@@ -155,10 +158,8 @@ def tile_attend_bsharedpower_s_kernel(tc, query, keys_words, keys_scales, pw, go
         xp = tile([P, I], F32, "xp")
         page_sum = tile([P, G], F32, "page_sum")
 
-        keys = [gather_words(key_words, h, "keys") for h in range(HALVES)]
-        old_sb = tile([P, T], F32, "old_sb", tag="key_words")
-        nc.sync.dma_start(out=old_sb[:], in_=old)
-        scores = [product(query_mx, keys[h], key_scale, h, "scores") for h in range(HALVES)]
+        keys = [gather_words(key_words, h, "keys", ["val_bytes", "key_bytes"][h]) for h in range(HALVES)]
+        scores = [product(query_mx, keys[h], key_scale, 0, h, "scores") for h in range(HALVES)]
         for h in range(HALVES):
             nc.vector.tensor_reduce(out=pages(page_max, h), in_=by_page(scores[h][:]), axis=AX.X, op=ALU.max)
         for h in range(HALVES):
@@ -178,7 +179,7 @@ def tile_attend_bsharedpower_s_kernel(tc, query, keys_words, keys_scales, pw, go
         for h in range(HALVES):
             nc.vector.tensor_reduce(out=pages(page_sum, h), in_=by_page(slots(x, h)), axis=AX.X, op=ALU.add)
             vals.append(gather_words(val_words, h, "vals"))
-        grads = [product(gout_mx, vals[h], val_scale, h, "grads") for h in range(HALVES)]
+        grads = [product(gout_mx, vals[h], val_scale, 4, h, "grads") for h in range(HALVES)]
 
         inv_guess = tile([P, G], F32, "inv_guess")
         guess = tile([P, G], F32, "guess")

@@ -1,4 +1,3 @@
-import math
 from contextlib import ExitStack
 
 import concourse.mybir as mybir
@@ -25,30 +24,6 @@ STORE_WIDTHS = [256, 512, 512, 512, 256]
 
 FLOPS = 2 * Q * I * (D + E)
 
-GUESS_TOP = 2.28125
-GUESS_DROP = 3.08
-GUESS_RATE = 0.318
-GUESS_REACH = 0.045
-LOG_DEGREE = 5
-
-
-def log_polynomial(reach, degree):
-    lo, hi = math.exp(-reach), math.exp(reach)
-    nodes = [(lo + hi) / 2 + (hi - lo) / 2 * math.cos(math.pi * (k + 0.5) / (degree + 1)) for k in range(degree + 1)]
-    diffs = [math.log(node) for node in nodes]
-    for level in range(1, degree + 1):
-        diffs = diffs[:level] + [(diffs[k] - diffs[k - 1]) / (nodes[k] - nodes[k - level]) for k in range(level, degree + 1)]
-    coeffs = [diffs[degree]]
-    for k in reversed(range(degree)):
-        coeffs = [up - nodes[k] * low for up, low in zip([diffs[k]] + coeffs, coeffs + [0.0])]
-    return coeffs
-
-
-LOG_COEFFS = log_polynomial(GUESS_REACH, LOG_DEGREE)
-SERIES_LEAD = LOG_COEFFS[LOG_DEGREE]
-SERIES_STEPS = [LOG_COEFFS[k] / SERIES_LEAD for k in reversed(range(1, LOG_DEGREE))]
-SERIES_CONST = LOG_COEFFS[0]
-
 
 def tile_attend_bsharedpower_s_kernel(tc, query, keys_words, keys_scales, pw, gout, vals_words, vals_scales, old, offs, out):
     nc = tc.nc
@@ -67,8 +42,8 @@ def tile_attend_bsharedpower_s_kernel(tc, query, keys_words, keys_scales, pw, go
         query_raw = tile([P, 4, Q], F32, "query_raw")
         gout_raw = tile([P, 4, Q], F32, "gout_raw")
         old_sb = tile([P, T], F32, "old_sb")
-        power = tile([P, 1], F32, "power")
         placed = tile([P, T], F32, "placed")
+        power = tile([P, 1], F32, "power")
 
         def load_scale_rows(dst, src, queue, first):
             for quad in range(4):
@@ -86,16 +61,17 @@ def tile_attend_bsharedpower_s_kernel(tc, query, keys_words, keys_scales, pw, go
         load_rows(query_raw, query, nc.sync)
         load_scale_rows(key_bytes, keys_scales, nc.sync, 0)
         load_words(key_words, keys_words)
-        load_scale_rows(val_bytes, vals_scales, nc.scalar, 4)
+        load_scale_rows(val_bytes, vals_scales, nc.sync, 4)
         load_rows(gout_raw, gout, nc.sync)
         nc.sync.dma_start(out=power[:], in_=pw)
         load_words(val_words, vals_words)
         nc.sync.dma_start(out=old_sb[:], in_=old)
+
         nc.vector.memset(placed[:], 0.0)
 
-        def cast(raw, name, copy):
+        def cast(raw, name):
             grouped = tile([P, Q, 4], BF16, name)
-            copy(out=grouped[:], in_=raw[:].rearrange("p j w -> p w j"))
+            nc.scalar.activation(grouped[:], raw[:].rearrange("p j w -> p w j"), ACT.Copy)
             return grouped
 
         def quantize(grouped, name):
@@ -140,11 +116,10 @@ def tile_attend_bsharedpower_s_kernel(tc, query, keys_words, keys_scales, pw, go
         def spread(ap, n):
             return ap.unsqueeze(2).to_broadcast([P, n, PAGE])
 
-        query_bf = cast(query_raw, "query_bf", nc.scalar.copy)
+        query_bf = cast(query_raw, "query_bf")
         key_scale = gather_bytes(key_bytes, "key_scale")
         query_mx = quantize(query_bf, "query")
-        val_scale = gather_bytes(val_bytes, "val_scale")
-        gout_bf = cast(gout_raw, "gout_bf", nc.scalar.copy)
+        gout_bf = cast(gout_raw, "gout_bf")
 
         neg_power = tile([P, 1], F32, "neg_power")
         gains = tile([P, 2], F32, "gains")
@@ -158,12 +133,19 @@ def tile_attend_bsharedpower_s_kernel(tc, query, keys_words, keys_scales, pw, go
         xp = tile([P, I], F32, "xp")
         page_sum = tile([P, G], F32, "page_sum")
 
-        keys = [gather_words(key_words, h, "keys", ["val_bytes", "key_bytes"][h]) for h in range(HALVES)]
+        keys = [gather_words(key_words, h, "keys", ["key_bytes", None][h]) for h in range(HALVES)]
+        val_scale = tile([P, I], U8, "val_scale")
+
+        def gather_val_scale(h):
+            nc.vector.tensor_copy(slots(val_scale, h), val_bytes[:].indirect(offsets[:, h * (SLOTS // 16) : (h + 1) * (SLOTS // 16)]))
+
+        gather_val_scale(0)
         scores = [product(query_mx, keys[h], key_scale, 0, h, "scores") for h in range(HALVES)]
         for h in range(HALVES):
             nc.vector.tensor_reduce(out=pages(page_max, h), in_=by_page(scores[h][:]), axis=AX.X, op=ALU.max)
         for h in range(HALVES):
             nc.vector.tensor_tensor(by_page(slots(rel, h)), by_page(scores[h][:]), spread(pages(page_max, h), PAGES), ALU.subtract)
+        gather_val_scale(1)
         for h in range(HALVES):
             nc.scalar.activation(slots(x, h), slots(rel, h), ACT.Exp)
         for h in range(HALVES):
@@ -175,67 +157,46 @@ def tile_attend_bsharedpower_s_kernel(tc, query, keys_words, keys_scales, pw, go
         nc.scalar.activation(weight[:], page_max[:], ACT.Exp, bias=neg_max[:])
         gout_mx = quantize(gout_bf, "gout")
 
-        vals = []
         for h in range(HALVES):
             nc.vector.tensor_reduce(out=pages(page_sum, h), in_=by_page(slots(x, h)), axis=AX.X, op=ALU.add)
-            vals.append(gather_words(val_words, h, "vals"))
+        vals = [gather_words(val_words, h, "vals") for h in range(HALVES)]
         grads = [product(gout_mx, vals[h], val_scale, 4, h, "grads") for h in range(HALVES)]
 
-        inv_guess = tile([P, G], F32, "inv_guess")
-        guess = tile([P, G], F32, "guess")
-        decay = tile([P, G], F32, "decay")
-        nc.scalar.activation(decay[:], page_sum[:], ACT.Exp, scale=-GUESS_RATE)
-        nc.scalar.activation(inv_guess[:], decay[:], ACT.Exp, scale=GUESS_DROP, bias=-GUESS_TOP)
-        nc.scalar.activation(guess[:], decay[:], ACT.Copy, scale=-GUESS_DROP, bias=GUESS_TOP + SERIES_CONST)
-
-        pair = tile([P, 2, G], F32, "pair")
-        mass = pair[:, 1, :]
+        mass = tile([P, G], F32, "mass")
         z = tile([P, 1], F32, "z")
         inv_z = tile([P, 1], F32, "inv_z")
         gains_z = tile([P, 2], F32, "gains_z")
         cross_gain = tile([P, 1], F32, "cross_gain")
-        u = tile([P, G], F32, "u")
         cx = tile([P, I], F32, "cx")
         page_grad = tile([P, G], F32, "page_grad")
-        horner = [tile([P, G], F32, "horner" + str(k)) for k in range(len(SERIES_STEPS))]
         log_sum = tile([P, G], F32, "log_sum")
 
-        def series_step(k):
-            src = u if k == 0 else horner[k - 1]
-            nc.vector.scalar_tensor_tensor(horner[k][:], src[:], SERIES_STEPS[k], u[:], ALU.add, ALU.mult)
-
-        nc.vector.scalar_tensor_tensor(mass, page_sum[:], 1.0, weight[:], ALU.mult, ALU.mult, accum_out=z[:])
-        nc.vector.tensor_tensor(u[:], page_sum[:], inv_guess[:], ALU.mult)
+        nc.scalar.activation(log_sum[:], page_sum[:], ACT.Ln)
+        nc.vector.scalar_tensor_tensor(mass[:], page_sum[:], 1.0, weight[:], ALU.mult, ALU.mult, accum_out=z[:])
         nc.vector.reciprocal(inv_z[:], z[:])
-        series_step(0)
-        nc.vector.tensor_tensor(slots(cx, 0), grads[0][:], slots(xp, 0), ALU.mult)
-        series_step(1)
-        nc.vector.tensor_tensor(slots(cx, 1), grads[1][:], slots(xp, 1), ALU.mult)
-        series_step(2)
-        nc.vector.tensor_reduce(out=pages(page_grad, 0), in_=by_page(slots(cx, 0)), axis=AX.X, op=ALU.add)
-        series_step(3)
-        nc.vector.tensor_reduce(out=pages(page_grad, 1), in_=by_page(slots(cx, 1)), axis=AX.X, op=ALU.add)
-        nc.vector.scalar_tensor_tensor(log_sum[:], horner[-1][:], SERIES_LEAD, guess[:], ALU.mult, ALU.add)
-        nc.scalar.activation(gains_z[:], gains[:], ACT.Copy, scale=inv_z[:])
-        nc.scalar.activation(cross_gain[:], inv_z[:], ACT.Copy, scale=-GAIN)
+        nc.vector.tensor_scalar(gains_z[:], gains[:], inv_z[:], None, ALU.mult)
+        nc.vector.tensor_scalar(cross_gain[:], inv_z[:], inv_z[:], -GAIN, ALU.mult, ALU.mult)
+        for h in range(HALVES):
+            nc.vector.tensor_tensor(slots(cx, h), grads[h][:], slots(xp, h), ALU.mult)
+        for h in range(HALVES):
+            nc.vector.tensor_reduce(out=pages(page_grad, h), in_=by_page(slots(cx, h)), axis=AX.X, op=ALU.add)
         r = tile([P, G], F32, "r")
         nc.scalar.activation(r[:], log_sum[:], ACT.Exp, scale=neg_power[:])
+        x_row = tile([P, I], F32, "x_row", "log_sum")
+        for h in range(HALVES):
+            nc.scalar.activation(slots(x_row, h), scores[h][:], ACT.Exp, bias=neg_max[:])
 
-        cross = tile([P, G], F32, "cross")
-        nc.vector.scalar_tensor_tensor(pair[:, 0, :], page_grad[:], gains_z[:, 0:1], weight[:], ALU.mult, ALU.mult)
-        nc.vector.scalar_tensor_tensor(cross[:], page_grad[:], cross_gain[:], mass, ALU.mult, ALU.mult)
-
-        pair_r = tile([P, 2, G], F32, "pair_r")
+        mass_r = tile([P, G], F32, "mass_r", "vals1")
         cross_r = tile([P, G], F32, "cross_r")
         row_term = tile([P, 1], F32, "row_term")
         page_term = tile([P, G], F32, "page_term")
         own = tile([P, I], F32, "own")
         shared = tile([P, I], F32, "shared")
-        nc.vector.scalar_tensor_tensor(cross_r[:], r[:], inv_z[:], cross[:], ALU.mult, ALU.mult, accum_out=row_term[:])
-        nc.vector.tensor_tensor(pair_r[:], pair[:], r[:].unsqueeze(1).to_broadcast([P, 2, G]), ALU.mult)
-        nc.vector.scalar_tensor_tensor(page_term[:], weight[:], row_term[:], pair_r[:, 0, :], ALU.mult, ALU.add)
-        nc.vector.scalar_tensor_tensor(by_page(own[:]), by_page(cx[:]), gains_z[:, 1:2], spread(pair_r[:, 1, :], G), ALU.mult, ALU.mult)
-        nc.vector.tensor_tensor(by_page(shared[:]), by_page(x[:]), spread(page_term[:], G), ALU.mult)
+        nc.vector.tensor_tensor(mass_r[:], mass[:], r[:], ALU.mult)
+        nc.vector.scalar_tensor_tensor(cross_r[:], page_grad[:], cross_gain[:], mass_r[:], ALU.mult, ALU.mult, accum_out=row_term[:])
+        nc.vector.scalar_tensor_tensor(page_term[:], page_grad[:], gains_z[:, 0:1], r[:], ALU.mult, ALU.mult)
+        nc.vector.scalar_tensor_tensor(by_page(own[:]), by_page(cx[:]), gains_z[:, 1:2], spread(mass_r[:], G), ALU.mult, ALU.mult)
+        nc.vector.scalar_tensor_tensor(by_page(shared[:]), spread(page_term[:], G), row_term[:], by_page(x_row[:]), ALU.add, ALU.mult)
         nc.vector.tensor_tensor(placed[:].indirect(offsets[:]), own[:], shared[:], ALU.add)
 
         start = 0

@@ -16,10 +16,18 @@ AX = mybir.AxisListType
 P = 128
 D, E, T, I, Q, G = 512, 512, 2048, 512, 128, 64
 PAGE = I // G
-HALVES = 2
-SLOTS = I // HALVES
-PAGES = G // HALVES
+PACK = 4
+QUADRANT = 32
+LIST_ROWS = 16
 GAIN = 128.0
+
+HALVES = 2
+HALF_SLOTS = I // HALVES
+HALF_PAGES = G // HALVES
+
+KEY_SCALE_ROW = 0
+VAL_SCALE_ROW = 4
+
 STORE_WIDTHS = [256, 512, 512, 512, 256]
 
 FLOPS = 2 * Q * I * (D + E)
@@ -31,48 +39,48 @@ def tile_attend_bsharedpower_s_kernel(tc, query, keys_words, keys_scales, pw, go
         sb = ctx.enter_context(tc.tile_pool(name="sb", bufs=1))
         ps = ctx.enter_context(tc.psum_pool(name="ps", bufs=1))
 
-        def tile(shape, dtype, name, tag=None):
-            return sb.tile(shape, dtype, name=name, tag=tag or name, align_bytes=64)
+        def tile(shape, dtype, name, reuse=None):
+            return sb.tile(shape, dtype, name=name, tag=reuse or name, align_bytes=64)
 
-        offsets = sb.tile([P, I // 16], U16, name="offsets")
+        offsets = sb.tile([P, I // LIST_ROWS], U16, name="offsets")
         key_bytes = tile([P, T], U8, "key_bytes")
         val_bytes = tile([P, T], U8, "val_bytes")
         key_words = tile([P, T], I32, "key_words")
         val_words = tile([P, T], I32, "val_words")
-        query_raw = tile([P, 4, Q], F32, "query_raw")
-        gout_raw = tile([P, 4, Q], F32, "gout_raw")
+        query_raw = tile([P, PACK, Q], F32, "query_raw")
+        gout_raw = tile([P, PACK, Q], F32, "gout_raw")
         old_sb = tile([P, T], F32, "old_sb")
         placed = tile([P, T], F32, "placed")
         power = tile([P, 1], F32, "power")
 
         def load_scale_rows(dst, src, queue, first):
-            for quad in range(4):
-                queue.dma_start(out=dst[32 * quad + first : 32 * quad + first + 4, :].bitcast(I32), in_=src[0, 4 * quad : 4 * quad + 4, :].bitcast(I32))
+            for n in range(P // QUADRANT):
+                row = QUADRANT * n + first
+                queue.dma_start(out=dst[row : row + PACK, :].bitcast(I32), in_=src[0, PACK * n : PACK * (n + 1), :].bitcast(I32))
 
         def load_words(dst, src):
             nc.sync.dma_start(out=dst[:], in_=src[0].rearrange("p n t -> p (n t)").bitcast(I32))
 
-        def load_rows(dst, src, queue):
-            queue.dma_start(out=dst[:], in_=src.rearrange("(p j) w -> p j w", j=4))
+        def load_rows(dst, src):
+            nc.sync.dma_start(out=dst[:], in_=src.rearrange("(p j) w -> p j w", j=PACK))
 
         nc.vector.memset(key_bytes[:].bitcast(I32), 0)
         nc.vector.memset(val_bytes[:].bitcast(I32), 0)
+
         nc.sync.dma_start(offsets[:], offs)
-        load_rows(query_raw, query, nc.sync)
-        load_scale_rows(key_bytes, keys_scales, nc.sync, 0)
+        load_rows(query_raw, query)
+        load_scale_rows(key_bytes, keys_scales, nc.sync, KEY_SCALE_ROW)
         load_words(key_words, keys_words)
-        load_scale_rows(val_bytes, vals_scales, nc.sync, 4)
-        load_rows(gout_raw, gout, nc.sync)
+        load_scale_rows(val_bytes, vals_scales, nc.scalar, VAL_SCALE_ROW)
+        load_rows(gout_raw, gout)
         nc.sync.dma_start(out=power[:], in_=pw)
         load_words(val_words, vals_words)
         nc.sync.dma_start(out=old_sb[:], in_=old)
 
         nc.vector.memset(placed[:], 0.0)
 
-        def cast(raw, name):
-            grouped = tile([P, Q, 4], BF16, name)
-            nc.scalar.activation(grouped[:], raw[:].rearrange("p j w -> p w j"), ACT.Copy)
-            return grouped
+        def interleaved(raw):
+            return raw[:].rearrange("p j w -> p w j")
 
         def quantize(grouped, name):
             codes = tile([P, Q], U32, name + "_codes")
@@ -85,41 +93,45 @@ def tile_attend_bsharedpower_s_kernel(tc, query, keys_words, keys_scales, pw, go
             nc.vector.tensor_copy(picked[:], window[:].indirect(offsets[:]))
             return picked
 
-        def gather_words(window, half, name, tag=None):
-            picked = tile([P, SLOTS], U32, name + str(half), tag)
-            cols = SLOTS // 16
-            nc.vector.tensor_copy(picked[:], window[:].bitcast(U32).indirect(offsets[:, half * cols : (half + 1) * cols]))
+        def gather_words(window, half, name, reuse=None):
+            picked = tile([P, HALF_SLOTS], U32, name + str(half), reuse)
+            list_cols = HALF_SLOTS // LIST_ROWS
+            nc.vector.tensor_copy(picked[:], window[:].bitcast(U32).indirect(offsets[:, half * list_cols : (half + 1) * list_cols]))
             return picked
 
-        def product(rows, words, scale_bytes, first, half, name):
-            bank = ps.tile([P, SLOTS], F32, name=name + str(half))
+        def product(rows_mx, words, scale_bytes, first, half, name):
+            codes, scales = rows_mx
+            bank = ps.tile([P, HALF_SLOTS], F32, name=name + str(half))
             nc.tensor.matmul_mx(
                 out=bank[:],
-                lhsT=rows[0][:].bitcast(FP8X4),
-                lhsT_scale=rows[1][:],
+                lhsT=codes[:].bitcast(FP8X4),
+                lhsT_scale=scales[:],
                 rhs=words[:].bitcast(FP8X4),
-                rhs_scale=scale_bytes[first:, half * SLOTS : (half + 1) * SLOTS],
+                rhs_scale=scale_bytes[first:, half * HALF_SLOTS : (half + 1) * HALF_SLOTS],
                 start=True,
                 stop=True,
             )
             return bank
 
         def slots(t, half):
-            return t[:, half * SLOTS : (half + 1) * SLOTS]
+            return t[:, half * HALF_SLOTS : (half + 1) * HALF_SLOTS]
 
         def pages(t, half):
-            return t[:, half * PAGES : (half + 1) * PAGES]
+            return t[:, half * HALF_PAGES : (half + 1) * HALF_PAGES]
 
         def by_page(ap):
             return ap.rearrange("p (g j) -> p g j", j=PAGE)
 
-        def spread(ap, n):
-            return ap.unsqueeze(2).to_broadcast([P, n, PAGE])
+        def spread(ap, count):
+            return ap.unsqueeze(2).to_broadcast([P, count, PAGE])
 
-        query_bf = cast(query_raw, "query_bf")
-        key_scale = gather_bytes(key_bytes, "key_scale")
+        query_bf = tile([P, Q, PACK], BF16, "query_bf")
+        nc.vector.tensor_copy(query_bf[:], interleaved(query_raw))
         query_mx = quantize(query_bf, "query")
-        gout_bf = cast(gout_raw, "gout_bf")
+        key_scale = gather_bytes(key_bytes, "key_scale")
+        val_scale = gather_bytes(val_bytes, "val_scale")
+        gout_bf = tile([P, Q, PACK], BF16, "gout_bf")
+        nc.scalar.activation(gout_bf[:], interleaved(gout_raw), ACT.Copy)
 
         neg_power = tile([P, 1], F32, "neg_power")
         gains = tile([P, 2], F32, "gains")
@@ -130,37 +142,31 @@ def tile_attend_bsharedpower_s_kernel(tc, query, keys_words, keys_scales, pw, go
         page_max = tile([P, G], F32, "page_max")
         rel = tile([P, I], F32, "rel")
         x = tile([P, I], F32, "x")
-        xp = tile([P, I], F32, "xp")
+        x_pow = tile([P, I], F32, "x_pow")
         page_sum = tile([P, G], F32, "page_sum")
 
-        keys = [gather_words(key_words, h, "keys", ["key_bytes", None][h]) for h in range(HALVES)]
-        val_scale = tile([P, I], U8, "val_scale")
-
-        def gather_val_scale(h):
-            nc.vector.tensor_copy(slots(val_scale, h), val_bytes[:].indirect(offsets[:, h * (SLOTS // 16) : (h + 1) * (SLOTS // 16)]))
-
-        gather_val_scale(0)
-        scores = [product(query_mx, keys[h], key_scale, 0, h, "scores") for h in range(HALVES)]
+        scale_windows = ["val_bytes", "key_bytes"]
+        keys = [gather_words(key_words, h, "keys", scale_windows[h]) for h in range(HALVES)]
+        scores = [product(query_mx, keys[h], key_scale, KEY_SCALE_ROW, h, "scores") for h in range(HALVES)]
         for h in range(HALVES):
             nc.vector.tensor_reduce(out=pages(page_max, h), in_=by_page(scores[h][:]), axis=AX.X, op=ALU.max)
         for h in range(HALVES):
-            nc.vector.tensor_tensor(by_page(slots(rel, h)), by_page(scores[h][:]), spread(pages(page_max, h), PAGES), ALU.subtract)
-        gather_val_scale(1)
+            nc.vector.tensor_tensor(by_page(slots(rel, h)), by_page(scores[h][:]), spread(pages(page_max, h), HALF_PAGES), ALU.subtract)
         for h in range(HALVES):
             nc.scalar.activation(slots(x, h), slots(rel, h), ACT.Exp)
         for h in range(HALVES):
-            nc.scalar.activation(slots(xp, h), slots(rel, h), ACT.Exp, scale=power[:])
+            nc.scalar.activation(slots(x_pow, h), slots(rel, h), ACT.Exp, scale=power[:])
 
         neg_max = tile([P, 1], F32, "neg_max")
         nc.vector.tensor_reduce(out=neg_max[:], in_=page_max[:], axis=AX.X, op=ALU.max, negate=True)
-        weight = tile([P, G], F32, "weight")
-        nc.scalar.activation(weight[:], page_max[:], ACT.Exp, bias=neg_max[:])
+        page_weight = tile([P, G], F32, "page_weight")
+        nc.scalar.activation(page_weight[:], page_max[:], ACT.Exp, bias=neg_max[:])
         gout_mx = quantize(gout_bf, "gout")
 
         for h in range(HALVES):
             nc.vector.tensor_reduce(out=pages(page_sum, h), in_=by_page(slots(x, h)), axis=AX.X, op=ALU.add)
         vals = [gather_words(val_words, h, "vals") for h in range(HALVES)]
-        grads = [product(gout_mx, vals[h], val_scale, 4, h, "grads") for h in range(HALVES)]
+        grads = [product(gout_mx, vals[h], val_scale, VAL_SCALE_ROW, h, "grads") for h in range(HALVES)]
 
         mass = tile([P, G], F32, "mass")
         z = tile([P, 1], F32, "z")
@@ -172,30 +178,31 @@ def tile_attend_bsharedpower_s_kernel(tc, query, keys_words, keys_scales, pw, go
         log_sum = tile([P, G], F32, "log_sum")
 
         nc.scalar.activation(log_sum[:], page_sum[:], ACT.Ln)
-        nc.vector.scalar_tensor_tensor(mass[:], page_sum[:], 1.0, weight[:], ALU.mult, ALU.mult, accum_out=z[:])
+        nc.vector.scalar_tensor_tensor(mass[:], page_sum[:], 1.0, page_weight[:], ALU.mult, ALU.mult, accum_out=z[:])
         nc.vector.reciprocal(inv_z[:], z[:])
         nc.vector.tensor_scalar(gains_z[:], gains[:], inv_z[:], None, ALU.mult)
         nc.vector.tensor_scalar(cross_gain[:], inv_z[:], inv_z[:], -GAIN, ALU.mult, ALU.mult)
         for h in range(HALVES):
-            nc.vector.tensor_tensor(slots(cx, h), grads[h][:], slots(xp, h), ALU.mult)
+            nc.vector.tensor_tensor(slots(cx, h), grads[h][:], slots(x_pow, h), ALU.mult)
         for h in range(HALVES):
             nc.vector.tensor_reduce(out=pages(page_grad, h), in_=by_page(slots(cx, h)), axis=AX.X, op=ALU.add)
-        r = tile([P, G], F32, "r")
-        nc.scalar.activation(r[:], log_sum[:], ACT.Exp, scale=neg_power[:])
+        share_pow = tile([P, G], F32, "share_pow")
+        nc.scalar.activation(share_pow[:], log_sum[:], ACT.Exp, scale=neg_power[:])
+
         x_row = tile([P, I], F32, "x_row", "log_sum")
         for h in range(HALVES):
             nc.scalar.activation(slots(x_row, h), scores[h][:], ACT.Exp, bias=neg_max[:])
 
-        mass_r = tile([P, G], F32, "mass_r", "vals1")
-        cross_r = tile([P, G], F32, "cross_r")
+        mass_pow = tile([P, G], F32, "mass_pow", "x_pow")
+        cross = tile([P, G], F32, "cross")
         row_term = tile([P, 1], F32, "row_term")
         page_term = tile([P, G], F32, "page_term")
         own = tile([P, I], F32, "own")
         shared = tile([P, I], F32, "shared")
-        nc.vector.tensor_tensor(mass_r[:], mass[:], r[:], ALU.mult)
-        nc.vector.scalar_tensor_tensor(cross_r[:], page_grad[:], cross_gain[:], mass_r[:], ALU.mult, ALU.mult, accum_out=row_term[:])
-        nc.vector.scalar_tensor_tensor(page_term[:], page_grad[:], gains_z[:, 0:1], r[:], ALU.mult, ALU.mult)
-        nc.vector.scalar_tensor_tensor(by_page(own[:]), by_page(cx[:]), gains_z[:, 1:2], spread(mass_r[:], G), ALU.mult, ALU.mult)
+        nc.vector.tensor_tensor(mass_pow[:], mass[:], share_pow[:], ALU.mult)
+        nc.vector.scalar_tensor_tensor(cross[:], page_grad[:], cross_gain[:], mass_pow[:], ALU.mult, ALU.mult, accum_out=row_term[:])
+        nc.vector.scalar_tensor_tensor(page_term[:], page_grad[:], gains_z[:, 0:1], share_pow[:], ALU.mult, ALU.mult)
+        nc.vector.scalar_tensor_tensor(by_page(own[:]), by_page(cx[:]), gains_z[:, 1:2], spread(mass_pow[:], G), ALU.mult, ALU.mult)
         nc.vector.scalar_tensor_tensor(by_page(shared[:]), spread(page_term[:], G), row_term[:], by_page(x_row[:]), ALU.add, ALU.mult)
         nc.vector.tensor_tensor(placed[:].indirect(offsets[:]), own[:], shared[:], ALU.add)
 

from contextlib import ExitStack

import concourse.mybir as mybir

F32 = mybir.dt.float32
BF16 = mybir.dt.bfloat16
I32 = mybir.dt.int32
U32 = mybir.dt.uint32
U16 = mybir.dt.uint16
U8 = mybir.dt.uint8
FP8X4 = mybir.dt.float8_e4m3fn_x4
ALU = mybir.AluOpType
ACT = mybir.ActivationFunctionType
AX = mybir.AxisListType

P = 128
D, E, T, I, Q, G = 512, 512, 2048, 512, 128, 64
PAGE = I // G
PACK = 4
QUADRANT = 32
LIST_ROWS = 16
GAIN = 128.0

HALVES = 2
HALF_SLOTS = I // HALVES
HALF_PAGES = G // HALVES

KEY_SCALE_ROW = 0
VAL_SCALE_ROW = 4

STORE_WIDTHS = [256, 512, 512, 512, 256]

FLOPS = 2 * Q * I * (D + E)


def tile_attend_bsharedpower_s_kernel(tc, query, keys_words, keys_scales, pw, gout, vals_words, vals_scales, old, offs, out):
    nc = tc.nc
    with ExitStack() as ctx:
        sb = ctx.enter_context(tc.tile_pool(name="sb", bufs=1))
        ps = ctx.enter_context(tc.psum_pool(name="ps", bufs=1))

        def tile(shape, dtype, name, reuse=None):
            return sb.tile(shape, dtype, name=name, tag=reuse or name, align_bytes=64)

        offsets = sb.tile([P, I // LIST_ROWS], U16, name="offsets")
        key_bytes = tile([P, T], U8, "key_bytes")
        val_bytes = tile([P, T], U8, "val_bytes")
        key_words = tile([P, T], I32, "key_words")
        val_words = tile([P, T], I32, "val_words")
        query_raw = tile([P, PACK, Q], F32, "query_raw")
        gout_raw = tile([P, PACK, Q], F32, "gout_raw")
        old_sb = tile([P, T], F32, "old_sb")
        placed = tile([P, T], F32, "placed")
        power = tile([P, 1], F32, "power")

        def load_scale_rows(dst, src, queue, first):
            for n in range(P // QUADRANT):
                row = QUADRANT * n + first
                queue.dma_start(out=dst[row : row + PACK, :].bitcast(I32), in_=src[0, PACK * n : PACK * (n + 1), :].bitcast(I32))

        def load_words(dst, src):
            nc.sync.dma_start(out=dst[:], in_=src[0].rearrange("p n t -> p (n t)").bitcast(I32))

        def load_rows(dst, src):
            nc.sync.dma_start(out=dst[:], in_=src.rearrange("(p j) w -> p j w", j=PACK))

        nc.vector.memset(key_bytes[:].bitcast(I32), 0)
        nc.vector.memset(val_bytes[:].bitcast(I32), 0)

        nc.sync.dma_start(offsets[:], offs)
        load_rows(query_raw, query)
        load_scale_rows(key_bytes, keys_scales, nc.sync, KEY_SCALE_ROW)
        load_words(key_words, keys_words)
        load_scale_rows(val_bytes, vals_scales, nc.scalar, VAL_SCALE_ROW)
        load_rows(gout_raw, gout)
        nc.sync.dma_start(out=power[:], in_=pw)
        load_words(val_words, vals_words)
        nc.sync.dma_start(out=old_sb[:], in_=old)

        nc.vector.memset(placed[:], 0.0)

        def interleaved(raw):
            return raw[:].rearrange("p j w -> p w j")

        def quantize(grouped, name):
            codes = tile([P, Q], U32, name + "_codes")
            scales = tile([P, Q], U8, name + "_scales")
            nc.vector.quantize_mx(out=codes[:].bitcast(FP8X4), scales=scales[:], in_=grouped[:].rearrange("p w j -> p (w j)"))
            return codes, scales

        def gather_bytes(window, name):
            picked = tile([P, I], U8, name)
            nc.vector.tensor_copy(picked[:], window[:].indirect(offsets[:]))
            return picked

        def gather_words(window, half, name, reuse=None):
            picked = tile([P, HALF_SLOTS], U32, name + str(half), reuse)
            list_cols = HALF_SLOTS // LIST_ROWS
            nc.vector.tensor_copy(picked[:], window[:].bitcast(U32).indirect(offsets[:, half * list_cols : (half + 1) * list_cols]))
            return picked

        def product(rows_mx, words, scale_bytes, first, half, name):
            codes, scales = rows_mx
            bank = ps.tile([P, HALF_SLOTS], F32, name=name + str(half))
            nc.tensor.matmul_mx(
                out=bank[:],
                lhsT=codes[:].bitcast(FP8X4),
                lhsT_scale=scales[:],
                rhs=words[:].bitcast(FP8X4),
                rhs_scale=scale_bytes[first:, half * HALF_SLOTS : (half + 1) * HALF_SLOTS],
                start=True,
                stop=True,
            )
            return bank

        def slots(t, half):
            return t[:, half * HALF_SLOTS : (half + 1) * HALF_SLOTS]

        def pages(t, half):
            return t[:, half * HALF_PAGES : (half + 1) * HALF_PAGES]

        def by_page(ap):
            return ap.rearrange("p (g j) -> p g j", j=PAGE)

        def spread(ap, count):
            return ap.unsqueeze(2).to_broadcast([P, count, PAGE])

        query_bf = tile([P, Q, PACK], BF16, "query_bf")
        nc.vector.tensor_copy(query_bf[:], interleaved(query_raw))
        query_mx = quantize(query_bf, "query")
        key_scale = gather_bytes(key_bytes, "key_scale")
        val_scale = gather_bytes(val_bytes, "val_scale")
        gout_bf = tile([P, Q, PACK], BF16, "gout_bf")
        nc.scalar.activation(gout_bf[:], interleaved(gout_raw), ACT.Copy)

        neg_power = tile([P, 1], F32, "neg_power")
        gains = tile([P, 2], F32, "gains")
        nc.scalar.activation(neg_power[:], power[:], ACT.Copy, scale=-1.0)
        nc.scalar.activation(gains[:, 0:1], power[:], ACT.Copy, scale=-GAIN, bias=GAIN)
        nc.scalar.activation(gains[:, 1:2], power[:], ACT.Copy, scale=GAIN)

        page_max = tile([P, G], F32, "page_max")
        rel = tile([P, I], F32, "rel")
        x = tile([P, I], F32, "x")
        x_pow = tile([P, I], F32, "x_pow")
        page_sum = tile([P, G], F32, "page_sum")

        scale_windows = ["val_bytes", "key_bytes"]
        keys = [gather_words(key_words, h, "keys", scale_windows[h]) for h in range(HALVES)]
        scores = [product(query_mx, keys[h], key_scale, KEY_SCALE_ROW, h, "scores") for h in range(HALVES)]
        for h in range(HALVES):
            nc.vector.tensor_reduce(out=pages(page_max, h), in_=by_page(scores[h][:]), axis=AX.X, op=ALU.max)
        for h in range(HALVES):
            nc.vector.tensor_tensor(by_page(slots(rel, h)), by_page(scores[h][:]), spread(pages(page_max, h), HALF_PAGES), ALU.subtract)
        for h in range(HALVES):
            nc.scalar.activation(slots(x, h), slots(rel, h), ACT.Exp)
        for h in range(HALVES):
            nc.scalar.activation(slots(x_pow, h), slots(rel, h), ACT.Exp, scale=power[:])

        neg_max = tile([P, 1], F32, "neg_max")
        nc.vector.tensor_reduce(out=neg_max[:], in_=page_max[:], axis=AX.X, op=ALU.max, negate=True)
        page_weight = tile([P, G], F32, "page_weight")
        nc.scalar.activation(page_weight[:], page_max[:], ACT.Exp, bias=neg_max[:])
        gout_mx = quantize(gout_bf, "gout")

        for h in range(HALVES):
            nc.vector.tensor_reduce(out=pages(page_sum, h), in_=by_page(slots(x, h)), axis=AX.X, op=ALU.add)
        vals = [gather_words(val_words, h, "vals") for h in range(HALVES)]
        grads = [product(gout_mx, vals[h], val_scale, VAL_SCALE_ROW, h, "grads") for h in range(HALVES)]

        mass = tile([P, G], F32, "mass")
        z = tile([P, 1], F32, "z")
        inv_z = tile([P, 1], F32, "inv_z")
        gains_z = tile([P, 2], F32, "gains_z")
        cross_gain = tile([P, 1], F32, "cross_gain")
        cx = tile([P, I], F32, "cx")
        page_grad = tile([P, G], F32, "page_grad")
        log_sum = tile([P, G], F32, "log_sum")

        nc.scalar.activation(log_sum[:], page_sum[:], ACT.Ln)
        nc.vector.scalar_tensor_tensor(mass[:], page_sum[:], 1.0, page_weight[:], ALU.mult, ALU.mult, accum_out=z[:])
        nc.vector.reciprocal(inv_z[:], z[:])
        nc.vector.tensor_scalar(gains_z[:], gains[:], inv_z[:], None, ALU.mult)
        nc.vector.tensor_scalar(cross_gain[:], inv_z[:], inv_z[:], -GAIN, ALU.mult, ALU.mult)
        for h in range(HALVES):
            nc.vector.tensor_tensor(slots(cx, h), grads[h][:], slots(x_pow, h), ALU.mult)
        for h in range(HALVES):
            nc.vector.tensor_reduce(out=pages(page_grad, h), in_=by_page(slots(cx, h)), axis=AX.X, op=ALU.add)
        share_pow = tile([P, G], F32, "share_pow")
        nc.scalar.activation(share_pow[:], log_sum[:], ACT.Exp, scale=neg_power[:])

        x_row = tile([P, I], F32, "x_row", "log_sum")
        for h in range(HALVES):
            nc.scalar.activation(slots(x_row, h), scores[h][:], ACT.Exp, bias=neg_max[:])

        mass_pow = tile([P, G], F32, "mass_pow", "x_pow")
        cross = tile([P, G], F32, "cross")
        row_term = tile([P, 1], F32, "row_term")
        page_term = tile([P, G], F32, "page_term")
        own = tile([P, I], F32, "own")
        shared = tile([P, I], F32, "shared")
        nc.vector.tensor_tensor(mass_pow[:], mass[:], share_pow[:], ALU.mult)
        nc.vector.scalar_tensor_tensor(cross[:], page_grad[:], cross_gain[:], mass_pow[:], ALU.mult, ALU.mult, accum_out=row_term[:])
        nc.vector.scalar_tensor_tensor(page_term[:], page_grad[:], gains_z[:, 0:1], share_pow[:], ALU.mult, ALU.mult)
        nc.vector.scalar_tensor_tensor(by_page(own[:]), by_page(cx[:]), gains_z[:, 1:2], spread(mass_pow[:], G), ALU.mult, ALU.mult)
        nc.vector.scalar_tensor_tensor(by_page(shared[:]), spread(page_term[:], G), row_term[:], by_page(x_row[:]), ALU.add, ALU.mult)
        nc.vector.tensor_tensor(placed[:].indirect(offsets[:]), own[:], shared[:], ALU.add)

        start = 0
        for k, width in enumerate(STORE_WIDTHS):
            cols = slice(start, start + width)
            total = tile([P, width], F32, "total" + str(k))
            nc.vector.tensor_tensor(total[:], placed[:, cols], old_sb[:, cols], ALU.add)
            nc.sync.dma_start(out=out[:, cols], in_=total[:])
            start = start + width
